import numpy as np
import ml_dtypes


def mxq(x, axis, fmt="e4m3"):
    dtype, down = {"e4m3": (ml_dtypes.float8_e4m3fn, 7), "e5m2": (ml_dtypes.float8_e5m2, 14)}[fmt]
    v = np.moveaxis(np.asarray(x, np.float32).astype(ml_dtypes.bfloat16).astype(np.float64), axis, -1)
    blocks = v.reshape(v.shape[:-1] + (-1, 32))
    amax = np.abs(blocks).max(-1, keepdims=True)
    byte = np.maximum(np.where(amax > 0, np.frexp(amax)[1] - 1 + 127, 0) - down, 1)
    scale = np.exp2(byte - 127.0)
    codes = (blocks / scale).astype(np.float32).astype(dtype).astype(np.float64)
    return np.moveaxis((codes * scale).reshape(v.shape), -1, axis)


WIDE = False


def mx_kscale(k, group=512):
    if not WIDE:
        return np.ones(k)
    levels = np.array([18, -18])
    if group != 512:
        return np.exp2(np.random.permutation(np.resize(levels, k // group))).repeat(group)
    if k % 512:
        return np.exp2(np.random.permutation(np.resize(levels, k // 32))).repeat(32)
    a = np.empty((k // 512, 16))
    for p in range(k // 512):
        a[p, :8] = np.random.permutation(np.resize(levels, 8))
        for g in range(8):
            far = levels[np.abs(levels - a[p, g]) >= 10]
            a[p, g + 8] = far[np.random.randint(len(far))]
    return np.exp2(a.ravel()).repeat(32)


def f64(x):
    return np.asarray(x).astype(np.float64)


G, D, I, Q, E = 8, 128, 128, 128, 128


def sgn(shape):
    return np.random.uniform(0.5, 2.0, shape) * np.where(np.random.standard_normal(shape) < 0, -1.0, 1.0)


def setup_inputs():
    n = np.random.standard_normal
    s_d = mx_kscale(D, 0)
    s_i = mx_kscale(I, 0)
    return {
        "kT": (n((G, D, I)) / np.sqrt(D) / s_d[:, None]).astype(np.float32),
        "qT": (n((G, D, Q)) * s_d[:, None]).astype(np.float32),
        "dk": (np.exp(-np.random.uniform(0.0, 3.0, (G, I, Q))) * (np.arange(I)[:, None] <= np.arange(Q)[None])).astype(np.float32),
        "t": (sgn((G, I, 1)) * s_i[:, None]).astype(np.float32),
        "v": ((n((G, I, E))) / s_i[:, None]).astype(np.float32),
        "S": (n((G, D, E)) / np.sqrt(D) / s_d[:, None]).astype(np.float32),
        "dq": (np.random.uniform(0.05, 1.0, (G, Q, 1))).astype(np.float32),
    }


def reference(kT, qT, dk, t, v, S, dq):
    kTq = mxq(f64(kT), 1, "e4m3")
    qTq = mxq(f64(qT), 1, "e4m3")
    z = kTq.transpose(0, 2, 1) @ qTq
    p = z * f64(dk) * f64(t)
    pq = mxq(p, 1, "e4m3")
    vq = mxq(f64(v), 1, "e4m3")
    y = pq.transpose(0, 2, 1) @ vq
    Sq = mxq(f64(S), 1, "e4m3")
    ys = qTq.transpose(0, 2, 1) @ Sq
    o = y + f64(dq) * ys
    return o

@@ -1,0 +1,175 @@
+from contextlib import ExitStack
+
+import concourse.mybir as mybir
+
+G, D, I, Q, E = 8, 128, 128, 128, 128
+FLOPS = 3 * 2 * G * 128 * 128 * 128
+
+F32 = mybir.dt.float32
+BF16 = mybir.dt.bfloat16
+U32 = mybir.dt.uint32
+U8 = mybir.dt.uint8
+FP8X4 = mybir.dt.float8_e4m3fn_x4
+MULT = mybir.AluOpType.mult
+ADD = mybir.AluOpType.add
+COPY = mybir.ActivationFunctionType.Copy
+
+P = 128
+PACK = 4
+ROWS = 32
+SIDE = 4
+SETS = 2
+W = 128
+
+
+def tile_rows_win_ssd_kernel(tc, kT, qT, dk, t, v, S, dq, out):
+    nc = tc.nc
+    with ExitStack() as ctx:
+        sb = ctx.enter_context(tc.tile_pool(name="sb", bufs=1))
+        ps = ctx.enter_context(tc.psum_pool(name="ps", bufs=1))
+        ctx.enter_context(tc.manual_schedule())
+
+        def load_packed(src, s, name):
+            raw = sb.tile([P, PACK, W], F32, name=name + "_raw%d" % s)
+            nc.sync.dma_start(
+                out=raw[:],
+                in_=src[SIDE * s : SIDE * (s + 1)].rearrange("g (p j) w -> (g p) j w", j=PACK),
+            )
+            return raw
+
+        def load_decay(s):
+            raw = sb.tile([P, SIDE, W], F32, name="dk_raw%d" % s)
+            nc.sync.dma_start(out=raw[:], in_=dk[SIDE * s : SIDE * (s + 1)].rearrange("g i q -> i g q"))
+            return raw
+
+        def interleave(on_vector, raw, name):
+            grouped = sb.tile([P, W, PACK], BF16, name=name + "_grp", align_bytes=64)
+            src = raw[:].rearrange("p j w -> p w j")
+            if on_vector:
+                nc.vector.tensor_copy(out=grouped[:], in_=src)
+            else:
+                nc.scalar.copy(out=grouped[:], in_=src)
+            return grouped
+
+        def quantize(grouped, name):
+            codes = sb.tile([P, W], U32, name=name + "_codes", align_bytes=64)
+            scales = sb.tile([P, W], U8, name=name + "_scales", align_bytes=64)
+            nc.vector.quantize_mx(
+                out=codes[:].bitcast(FP8X4),
+                scales=scales[:],
+                in_=grouped[:].rearrange("p w j -> p (w j)"),
+            )
+            return codes, scales
+
+        def products(dsts, stationary, moving):
+            for r in range(SIDE):
+                rows = slice(ROWS * r, ROWS * (r + 1))
+                nc.tensor.matmul_mx(
+                    out=dsts[r],
+                    lhsT=stationary[0][rows, :].bitcast(FP8X4),
+                    lhsT_scale=stationary[1][rows, :],
+                    rhs=moving[0][rows, :].bitcast(FP8X4),
+                    rhs_scale=moving[1][rows, :],
+                    start=True,
+                    stop=True,
+                )
+
+        bank_a = []
+        bank_b = []
+        for r in range(SIDE):
+            a_tile = ps.tile([P, 4, W], F32, name="bank_a%d" % r)
+            b_tile = ps.tile([P, 4, W], F32, name="bank_b%d" % r)
+            bank_a.append(a_tile)
+            bank_b.append(b_tile)
+
+        rows_in = sb.tile([P, G, ROWS], F32, name="rows_in", align_bytes=64)
+        cols = sb.tile([P, G, ROWS], F32, name="cols", align_bytes=64)
+        nc.vector.memset(rows_in[:], 0.0)
+        nc.scalar.dma_start(out=rows_in[0:P:ROWS], in_=t.rearrange("g (a b) o -> a g (b o)", b=ROWS))
+        nc.scalar.dma_start(out=rows_in[1:P:ROWS], in_=dq.rearrange("g (a b) o -> a g (b o)", b=ROWS))
+
+        k_raw0 = load_packed(kT, 0, "k")
+        q_raw0 = load_packed(qT, 0, "q")
+        k_raw1 = load_packed(kT, 1, "k")
+        q_raw1 = load_packed(qT, 1, "q")
+        decay = [load_decay(0), load_decay(1)]
+        s_raw0 = load_packed(S, 0, "s")
+        v_raw0 = load_packed(v, 0, "v")
+
+        def weights(s):
+            p_rows = sb.tile([P, SIDE, W], BF16, name="p_rows%d" % s)
+            for r in range(SIDE):
+                nc.vector.scalar_tensor_tensor(
+                    out=p_rows[:, r, :],
+                    in0=bank_a[r][:, s, :],
+                    scalar=cols[:, SIDE * s + r, 0:1],
+                    in1=decay[s][:, r, :],
+                    op0=MULT,
+                    op1=MULT,
+                )
+            return p_rows
+
+        def to_row_tiles(p_rows, s):
+            p_raw = sb.tile([P, PACK, W], BF16, name="p_raw%d" % s)
+            for r in (0, 2, 1, 3):
+                nc.sync.dma_start(out=p_raw[ROWS * r : ROWS * (r + 1)], in_=p_rows[:, r, :])
+            return p_raw
+
+        def scale_state_term(s):
+            carried = sb.tile([P, SIDE, W], F32, name="carried%d" % s)
+            for r in range(SIDE):
+                nc.scalar.activation(
+                    out=carried[:, r, :], in_=bank_b[r][:, s, :], func=COPY, scale=cols[:, SIDE * s + r, 1:2]
+                )
+            return carried
+
+        def finish(s, carried, bank, slot):
+            res = sb.tile([P, SIDE, W], F32, name="res%d" % s)
+            for r in range(SIDE):
+                nc.vector.tensor_tensor(out=res[:, r, :], in0=bank[r][:, slot, :], in1=carried[:, r, :], op=ADD)
+                if r % 2 == 1:
+                    g0 = SIDE * s + r - 1
+                    nc.sync.dma_start(
+                        out=out[g0 : g0 + 2].rearrange("g q e -> q g e"), in_=res[:, r - 1 : r + 1, :]
+                    )
+
+        k_grp0 = interleave(False, k_raw0, "k0")
+        q_grp0 = interleave(True, q_raw0, "q0")
+        k_mx0 = quantize(k_grp0, "k0")
+        q_mx0 = quantize(q_grp0, "q0")
+        products([b[:, 0, :] for b in bank_a], k_mx0, q_mx0)
+        k_grp1 = interleave(False, k_raw1, "k1")
+        nc.vector.transpose(
+            out=cols[:].rearrange("p g b -> p (g b)"), in_=rows_in[:].rearrange("p g b -> p (g b)")
+        )
+        q_grp1 = interleave(True, q_raw1, "q1")
+        k_mx1 = quantize(k_grp1, "k1")
+        q_mx1 = quantize(q_grp1, "q1")
+        p_rows0 = weights(0)
+        products([b[:, 1, :] for b in bank_a], k_mx1, q_mx1)
+        p_raw0 = to_row_tiles(p_rows0, 0)
+        s_raw1 = load_packed(S, 1, "s")
+        v_raw1 = load_packed(v, 1, "v")
+        p_rows1 = weights(1)
+        p_raw1 = to_row_tiles(p_rows1, 1)
+
+        s_grp0 = interleave(False, s_raw0, "s0")
+        v_grp0 = interleave(False, v_raw0, "v0")
+        s_mx0 = quantize(s_grp0, "s0")
+        products([b[:, 0, :] for b in bank_b], q_mx0, s_mx0)
+        p_grp0 = interleave(True, p_raw0, "p0")
+        v_mx0 = quantize(v_grp0, "v0")
+        p_mx0 = quantize(p_grp0, "p0")
+        carried0 = scale_state_term(0)
+        products([b[:, 2, :] for b in bank_a], p_mx0, v_mx0)
+        s_grp1 = interleave(False, s_raw1, "s1")
+        v_grp1 = interleave(True, v_raw1, "v1")
+        s_mx1 = quantize(s_grp1, "s1")
+        products([b[:, 1, :] for b in bank_b], q_mx1, s_mx1)
+        finish(0, carried0, bank_a, 2)
+        carried1 = scale_state_term(1)
+        p_grp1 = interleave(True, p_raw1, "p1")
+        v_mx1 = quantize(v_grp1, "v1")
+        p_mx1 = quantize(p_grp1, "p1")
+        products([b[:, 3, :] for b in bank_a], p_mx1, v_mx1)
+        finish(1, carried1, bank_a, 3)

@@ -20,6 +20,7 @@ ROWS = 32
 SIDE = 4
 SETS = 2
 W = 128
+SPLIT = 80
 
 
 def tile_rows_win_ssd_kernel(tc, kT, qT, dk, t, v, S, dq, out):
@@ -44,11 +45,18 @@ def tile_rows_win_ssd_kernel(tc, kT, qT, dk, t, v, S, dq, out):
 
         def interleave(on_vector, raw, name):
             grouped = sb.tile([P, W, PACK], BF16, name=name + "_grp", align_bytes=64)
-            src = raw[:].rearrange("p j w -> p w j")
+            src = raw[:, :, :].rearrange("p j w -> p w j")
             if on_vector:
                 nc.vector.tensor_copy(out=grouped[:], in_=src)
             else:
                 nc.scalar.copy(out=grouped[:], in_=src)
+            return grouped
+
+        def interleave_shared(raw, name):
+            grouped = sb.tile([P, W, PACK], BF16, name=name + "_grp", align_bytes=64)
+            src = raw[:, :, :].rearrange("p j w -> p w j")
+            nc.vector.tensor_copy(out=grouped[:, 0:SPLIT, :], in_=src[:, 0:SPLIT, :])
+            nc.scalar.copy(out=grouped[:, SPLIT:W, :], in_=src[:, SPLIT:W, :])
             return grouped
 
         def quantize(grouped, name):
@@ -62,7 +70,7 @@ def tile_rows_win_ssd_kernel(tc, kT, qT, dk, t, v, S, dq, out):
             return codes, scales
 
         def products(dsts, stationary, moving):
-            for r in range(SIDE):
+            for r in (0, 2, 1, 3):
                 rows = slice(ROWS * r, ROWS * (r + 1))
                 nc.tensor.matmul_mx(
                     out=dsts[r],
@@ -85,41 +93,37 @@ def tile_rows_win_ssd_kernel(tc, kT, qT, dk, t, v, S, dq, out):
         rows_in = sb.tile([P, G, ROWS], F32, name="rows_in", align_bytes=64)
         cols = sb.tile([P, G, ROWS], F32, name="cols", align_bytes=64)
         nc.vector.memset(rows_in[:], 0.0)
-        nc.scalar.dma_start(out=rows_in[0:P:ROWS], in_=t.rearrange("g (a b) o -> a g (b o)", b=ROWS))
-        nc.scalar.dma_start(out=rows_in[1:P:ROWS], in_=dq.rearrange("g (a b) o -> a g (b o)", b=ROWS))
 
         k_raw0 = load_packed(kT, 0, "k")
         q_raw0 = load_packed(qT, 0, "q")
+        nc.sync.dma_start(out=rows_in[0:P:ROWS], in_=t.rearrange("g (a b) o -> a g (b o)", b=ROWS))
+        nc.sync.dma_start(out=rows_in[1:P:ROWS], in_=dq.rearrange("g (a b) o -> a g (b o)", b=ROWS))
         k_raw1 = load_packed(kT, 1, "k")
         q_raw1 = load_packed(qT, 1, "q")
         decay = [load_decay(0), load_decay(1)]
         s_raw0 = load_packed(S, 0, "s")
+        s_raw1 = load_packed(S, 1, "s")
         v_raw0 = load_packed(v, 0, "v")
+        v_raw1 = load_packed(v, 1, "v")
 
-        def weights(s):
-            p_rows = sb.tile([P, SIDE, W], BF16, name="p_rows%d" % s)
-            for r in range(SIDE):
-                nc.vector.scalar_tensor_tensor(
-                    out=p_rows[:, r, :],
-                    in0=bank_a[r][:, s, :],
-                    scalar=cols[:, SIDE * s + r, 0:1],
-                    in1=decay[s][:, r, :],
-                    op0=MULT,
-                    op1=MULT,
-                )
-            return p_rows
+        p_rows = sb.tile([P, SIDE, SETS * W], BF16, name="p_rows")
+        p_raw = sb.tile([P, PACK, SETS * W], BF16, name="p_raw")
 
-        def to_row_tiles(p_rows, s):
-            p_raw = sb.tile([P, PACK, W], BF16, name="p_raw%d" % s)
-            for r in (0, 2, 1, 3):
-                nc.sync.dma_start(out=p_raw[ROWS * r : ROWS * (r + 1)], in_=p_rows[:, r, :])
-            return p_raw
+        def weights(s, r):
+            nc.vector.scalar_tensor_tensor(
+                out=p_rows[:, r, s * W : (s + 1) * W],
+                in0=(bank_a, bank_b)[s][r][:, 0, :],
+                scalar=cols[:, SIDE * s + r, 0:1],
+                in1=decay[s][:, r, :],
+                op0=MULT,
+                op1=MULT,
+            )
 
         def scale_state_term(s):
             carried = sb.tile([P, SIDE, W], F32, name="carried%d" % s)
             for r in range(SIDE):
                 nc.scalar.activation(
-                    out=carried[:, r, :], in_=bank_b[r][:, s, :], func=COPY, scale=cols[:, SIDE * s + r, 1:2]
+                    out=carried[:, r, :], in_=(bank_a, bank_b)[s][r][:, 1, :], func=COPY, scale=cols[:, SIDE * s + r, 1:2]
                 )
             return carried
 
@@ -133,43 +137,42 @@ def tile_rows_win_ssd_kernel(tc, kT, qT, dk, t, v, S, dq, out):
                         out=out[g0 : g0 + 2].rearrange("g q e -> q g e"), in_=res[:, r - 1 : r + 1, :]
                     )
 
-        k_grp0 = interleave(False, k_raw0, "k0")
+        k_grp0 = interleave(True, k_raw0, "k0")
         q_grp0 = interleave(True, q_raw0, "q0")
         k_mx0 = quantize(k_grp0, "k0")
+        k_grp1 = interleave(False, k_raw1, "k1")
         q_mx0 = quantize(q_grp0, "q0")
         products([b[:, 0, :] for b in bank_a], k_mx0, q_mx0)
-        k_grp1 = interleave(False, k_raw1, "k1")
         nc.vector.transpose(
             out=cols[:].rearrange("p g b -> p (g b)"), in_=rows_in[:].rearrange("p g b -> p (g b)")
         )
-        q_grp1 = interleave(True, q_raw1, "q1")
+        q_grp1 = interleave_shared(q_raw1, "q1")
         k_mx1 = quantize(k_grp1, "k1")
         q_mx1 = quantize(q_grp1, "q1")
-        p_rows0 = weights(0)
-        products([b[:, 1, :] for b in bank_a], k_mx1, q_mx1)
-        p_raw0 = to_row_tiles(p_rows0, 0)
-        s_raw1 = load_packed(S, 1, "s")
-        v_raw1 = load_packed(v, 1, "v")
-        p_rows1 = weights(1)
-        p_raw1 = to_row_tiles(p_rows1, 1)
+        products([b[:, 0, :] for b in bank_b], k_mx1, q_mx1)
+        for r in (0, 2, 1, 3):
+            weights(0, r)
+        for r in (0, 2, 1, 3):
+            weights(1, r)
+            nc.sync.dma_start(out=p_raw[ROWS * r : ROWS * (r + 1)], in_=p_rows[:, r, :])
 
         s_grp0 = interleave(False, s_raw0, "s0")
-        v_grp0 = interleave(False, v_raw0, "v0")
-        s_mx0 = quantize(s_grp0, "s0")
-        products([b[:, 0, :] for b in bank_b], q_mx0, s_mx0)
-        p_grp0 = interleave(True, p_raw0, "p0")
-        v_mx0 = quantize(v_grp0, "v0")
-        p_mx0 = quantize(p_grp0, "p0")
-        carried0 = scale_state_term(0)
-        products([b[:, 2, :] for b in bank_a], p_mx0, v_mx0)
         s_grp1 = interleave(False, s_raw1, "s1")
-        v_grp1 = interleave(True, v_raw1, "v1")
+        s_mx0 = quantize(s_grp0, "s0")
+        products([b[:, 1, :] for b in bank_a], q_mx0, s_mx0)
+        v_grp0 = interleave(True, v_raw0, "v0")
         s_mx1 = quantize(s_grp1, "s1")
         products([b[:, 1, :] for b in bank_b], q_mx1, s_mx1)
-        finish(0, carried0, bank_a, 2)
-        carried1 = scale_state_term(1)
-        p_grp1 = interleave(True, p_raw1, "p1")
+        v_grp1 = interleave(True, v_raw1, "v1")
+        v_mx0 = quantize(v_grp0, "v0")
+        carried0 = scale_state_term(0)
         v_mx1 = quantize(v_grp1, "v1")
+        p_grp0 = interleave(True, p_raw[:, :, 0:W], "p0")
+        p_grp1 = interleave(False, p_raw[:, :, W : 2 * W], "p1")
+        carried1 = scale_state_term(1)
+        p_mx0 = quantize(p_grp0, "p0")
+        products([b[:, 2, :] for b in bank_a], p_mx0, v_mx0)
         p_mx1 = quantize(p_grp1, "p1")
-        products([b[:, 3, :] for b in bank_a], p_mx1, v_mx1)
-        finish(1, carried1, bank_a, 3)
+        products([b[:, 2, :] for b in bank_b], p_mx1, v_mx1)
+        finish(0, carried0, bank_a, 2)
+        finish(1, carried1, bank_b, 2)

@@ -21,6 +21,8 @@ SIDE = 4
 SETS = 2
 W = 128
 SPLIT = 80
+RUN = 4
+TILE_ORDER = (0, 2, 1, 3)
 
 
 def tile_rows_win_ssd_kernel(tc, kT, qT, dk, t, v, S, dq, out):
@@ -43,20 +45,15 @@ def tile_rows_win_ssd_kernel(tc, kT, qT, dk, t, v, S, dq, out):
             nc.sync.dma_start(out=raw[:], in_=dk[SIDE * s : SIDE * (s + 1)].rearrange("g i q -> i g q"))
             return raw
 
-        def interleave(on_vector, raw, name):
+        def interleave(raw, name, vector_cols):
             grouped = sb.tile([P, W, PACK], BF16, name=name + "_grp", align_bytes=64)
-            src = raw[:, :, :].rearrange("p j w -> p w j")
-            if on_vector:
-                nc.vector.tensor_copy(out=grouped[:], in_=src)
-            else:
-                nc.scalar.copy(out=grouped[:], in_=src)
-            return grouped
-
-        def interleave_shared(raw, name):
-            grouped = sb.tile([P, W, PACK], BF16, name=name + "_grp", align_bytes=64)
-            src = raw[:, :, :].rearrange("p j w -> p w j")
-            nc.vector.tensor_copy(out=grouped[:, 0:SPLIT, :], in_=src[:, 0:SPLIT, :])
-            nc.scalar.copy(out=grouped[:, SPLIT:W, :], in_=src[:, SPLIT:W, :])
+            src = raw[:, :, :].rearrange("p j (c i) -> p c j i", i=RUN)
+            dst = grouped[:].rearrange("p (c i) j -> p c j i", i=RUN)
+            cut = vector_cols // RUN
+            if vector_cols > 0:
+                nc.vector.tensor_copy(out=dst[:, 0:cut], in_=src[:, 0:cut])
+            if vector_cols < W:
+                nc.scalar.copy(out=dst[:, cut:], in_=src[:, cut:])
             return grouped
 
         def quantize(grouped, name):
@@ -69,11 +66,19 @@ def tile_rows_win_ssd_kernel(tc, kT, qT, dk, t, v, S, dq, out):
             )
             return codes, scales
 
-        def products(dsts, stationary, moving):
-            for r in (0, 2, 1, 3):
+        banks = []
+        for s in range(SETS):
+            row = []
+            for r in range(SIDE):
+                bank = ps.tile([P, 4, W], F32, name="bank%d_%d" % (s, r))
+                row.append(bank)
+            banks.append(row)
+
+        def products(s, slot, stationary, moving, order):
+            for r in order:
                 rows = slice(ROWS * r, ROWS * (r + 1))
                 nc.tensor.matmul_mx(
-                    out=dsts[r],
+                    out=banks[s][r][:, slot, :],
                     lhsT=stationary[0][rows, :].bitcast(FP8X4),
                     lhsT_scale=stationary[1][rows, :],
                     rhs=moving[0][rows, :].bitcast(FP8X4),
@@ -82,97 +87,102 @@ def tile_rows_win_ssd_kernel(tc, kT, qT, dk, t, v, S, dq, out):
                     stop=True,
                 )
 
-        bank_a = []
-        bank_b = []
-        for r in range(SIDE):
-            a_tile = ps.tile([P, 4, W], F32, name="bank_a%d" % r)
-            b_tile = ps.tile([P, 4, W], F32, name="bank_b%d" % r)
-            bank_a.append(a_tile)
-            bank_b.append(b_tile)
+        t_rows = sb.tile([P, G, ROWS], F32, name="t_rows", align_bytes=64)
+        t_cols = sb.tile([P, G, ROWS], F32, name="t_cols", align_bytes=64)
+        dq_rows = sb.tile([P, G, ROWS], F32, name="dq_rows", align_bytes=64)
+        dq_cols = sb.tile([P, G, ROWS], F32, name="dq_cols", align_bytes=64)
+        nc.vector.memset(t_rows[:], 0.0)
+        nc.vector.memset(dq_rows[:], 0.0)
 
-        rows_in = sb.tile([P, G, ROWS], F32, name="rows_in", align_bytes=64)
-        cols = sb.tile([P, G, ROWS], F32, name="cols", align_bytes=64)
-        nc.vector.memset(rows_in[:], 0.0)
+        def load_rows(rows, src):
+            nc.sync.dma_start(out=rows[0:P:ROWS], in_=src.rearrange("g (a b) o -> a g (b o)", b=ROWS))
 
-        k_raw0 = load_packed(kT, 0, "k")
-        q_raw0 = load_packed(qT, 0, "q")
-        nc.sync.dma_start(out=rows_in[0:P:ROWS], in_=t.rearrange("g (a b) o -> a g (b o)", b=ROWS))
-        nc.sync.dma_start(out=rows_in[1:P:ROWS], in_=dq.rearrange("g (a b) o -> a g (b o)", b=ROWS))
-        k_raw1 = load_packed(kT, 1, "k")
-        q_raw1 = load_packed(qT, 1, "q")
-        decay = [load_decay(0), load_decay(1)]
-        s_raw0 = load_packed(S, 0, "s")
-        s_raw1 = load_packed(S, 1, "s")
-        v_raw0 = load_packed(v, 0, "v")
-        v_raw1 = load_packed(v, 1, "v")
+        def turn(cols, rows):
+            nc.vector.transpose(out=cols[:].rearrange("p g b -> p (g b)"), in_=rows[:].rearrange("p g b -> p (g b)"))
 
         p_rows = sb.tile([P, SIDE, SETS * W], BF16, name="p_rows")
         p_raw = sb.tile([P, PACK, SETS * W], BF16, name="p_raw")
+        carried = []
+        res = []
+        for s in range(SETS):
+            c_tile = sb.tile([P, SIDE, W], F32, name="carried%d" % s)
+            r_tile = sb.tile([P, SIDE, W], F32, name="res%d" % s)
+            carried.append(c_tile)
+            res.append(r_tile)
 
         def weights(s, r):
             nc.vector.scalar_tensor_tensor(
                 out=p_rows[:, r, s * W : (s + 1) * W],
-                in0=(bank_a, bank_b)[s][r][:, 0, :],
-                scalar=cols[:, SIDE * s + r, 0:1],
+                in0=banks[s][r][:, 0, :],
+                scalar=t_cols[:, SIDE * s + r, 0:1],
                 in1=decay[s][:, r, :],
                 op0=MULT,
                 op1=MULT,
             )
 
         def scale_state_term(s):
-            carried = sb.tile([P, SIDE, W], F32, name="carried%d" % s)
             for r in range(SIDE):
                 nc.scalar.activation(
-                    out=carried[:, r, :], in_=(bank_a, bank_b)[s][r][:, 1, :], func=COPY, scale=cols[:, SIDE * s + r, 1:2]
+                    out=carried[s][:, r, :], in_=banks[s][r][:, 1, :], func=COPY, scale=dq_cols[:, SIDE * s + r, 0:1]
                 )
-            return carried
 
-        def finish(s, carried, bank, slot):
-            res = sb.tile([P, SIDE, W], F32, name="res%d" % s)
-            for r in range(SIDE):
-                nc.vector.tensor_tensor(out=res[:, r, :], in0=bank[r][:, slot, :], in1=carried[:, r, :], op=ADD)
-                if r % 2 == 1:
-                    g0 = SIDE * s + r - 1
-                    nc.sync.dma_start(
-                        out=out[g0 : g0 + 2].rearrange("g q e -> q g e"), in_=res[:, r - 1 : r + 1, :]
-                    )
+        def add(s, r):
+            nc.vector.tensor_tensor(out=res[s][:, r, :], in0=banks[s][r][:, 2, :], in1=carried[s][:, r, :], op=ADD)
 
-        k_grp0 = interleave(True, k_raw0, "k0")
-        q_grp0 = interleave(True, q_raw0, "q0")
+        def store(s, r0, r1):
+            g0 = SIDE * s
+            nc.sync.dma_start(out=out[g0 + r0 : g0 + r1].rearrange("g q e -> q g e"), in_=res[s][:, r0:r1, :])
+
+        k_raw0 = load_packed(kT, 0, "k")
+        q_raw0 = load_packed(qT, 0, "q")
+        load_rows(t_rows, t)
+        k_raw1 = load_packed(kT, 1, "k")
+        q_raw1 = load_packed(qT, 1, "q")
+        decay = [load_decay(0), load_decay(1)]
+        s_raw0 = load_packed(S, 0, "s")
+        s_raw1 = load_packed(S, 1, "s")
+        load_rows(dq_rows, dq)
+        v_raw0 = load_packed(v, 0, "v")
+        v_raw1 = load_packed(v, 1, "v")
+
+        k_grp0 = interleave(k_raw0, "k0", W)
+        q_grp0 = interleave(q_raw0, "q0", 0)
         k_mx0 = quantize(k_grp0, "k0")
-        k_grp1 = interleave(False, k_raw1, "k1")
+        turn(t_cols, t_rows)
+        k_grp1 = interleave(k_raw1, "k1", W)
         q_mx0 = quantize(q_grp0, "q0")
-        products([b[:, 0, :] for b in bank_a], k_mx0, q_mx0)
-        nc.vector.transpose(
-            out=cols[:].rearrange("p g b -> p (g b)"), in_=rows_in[:].rearrange("p g b -> p (g b)")
-        )
-        q_grp1 = interleave_shared(q_raw1, "q1")
+        products(0, 0, k_mx0, q_mx0, TILE_ORDER)
+        q_grp1 = interleave(q_raw1, "q1", SPLIT)
         k_mx1 = quantize(k_grp1, "k1")
         q_mx1 = quantize(q_grp1, "q1")
-        products([b[:, 0, :] for b in bank_b], k_mx1, q_mx1)
-        for r in (0, 2, 1, 3):
+        products(1, 0, k_mx1, q_mx1, TILE_ORDER)
+        for r in TILE_ORDER:
             weights(0, r)
-        for r in (0, 2, 1, 3):
+        for r in TILE_ORDER:
             weights(1, r)
             nc.sync.dma_start(out=p_raw[ROWS * r : ROWS * (r + 1)], in_=p_rows[:, r, :])
 
-        s_grp0 = interleave(False, s_raw0, "s0")
-        s_grp1 = interleave(False, s_raw1, "s1")
+        s_grp0 = interleave(s_raw0, "s0", 0)
+        s_grp1 = interleave(s_raw1, "s1", W)
         s_mx0 = quantize(s_grp0, "s0")
-        products([b[:, 1, :] for b in bank_a], q_mx0, s_mx0)
-        v_grp0 = interleave(True, v_raw0, "v0")
+        products(0, 1, q_mx0, s_mx0, range(SIDE))
         s_mx1 = quantize(s_grp1, "s1")
-        products([b[:, 1, :] for b in bank_b], q_mx1, s_mx1)
-        v_grp1 = interleave(True, v_raw1, "v1")
+        products(1, 1, q_mx1, s_mx1, range(SIDE))
+        v_grp0 = interleave(v_raw0, "v0", 0)
+        turn(dq_cols, dq_rows)
+        v_grp1 = interleave(v_raw1, "v1", W)
         v_mx0 = quantize(v_grp0, "v0")
-        carried0 = scale_state_term(0)
+        scale_state_term(0)
         v_mx1 = quantize(v_grp1, "v1")
-        p_grp0 = interleave(True, p_raw[:, :, 0:W], "p0")
-        p_grp1 = interleave(False, p_raw[:, :, W : 2 * W], "p1")
-        carried1 = scale_state_term(1)
+        p_grp0 = interleave(p_raw[:, :, 0:W], "p0", SPLIT)
+        p_grp1 = interleave(p_raw[:, :, W : 2 * W], "p1", 0)
+        scale_state_term(1)
         p_mx0 = quantize(p_grp0, "p0")
-        products([b[:, 2, :] for b in bank_a], p_mx0, v_mx0)
+        products(0, 2, p_mx0, v_mx0, range(SIDE))
         p_mx1 = quantize(p_grp1, "p1")
-        products([b[:, 2, :] for b in bank_b], p_mx1, v_mx1)
-        finish(0, carried0, bank_a, 2)
-        finish(1, carried1, bank_b, 2)
+        products(1, 2, p_mx1, v_mx1, range(SIDE))
+        for s in range(SETS):
+            for r in range(SIDE):
+                add(s, r)
+                if r % 2 == 1:
+                    store(s, r - 1, r + 1)

from contextlib import ExitStack

import concourse.mybir as mybir

G, D, I, Q, E = 8, 128, 128, 128, 128
FLOPS = 3 * 2 * G * 128 * 128 * 128

F32 = mybir.dt.float32
BF16 = mybir.dt.bfloat16
U32 = mybir.dt.uint32
U8 = mybir.dt.uint8
FP8X4 = mybir.dt.float8_e4m3fn_x4
MULT = mybir.AluOpType.mult
ADD = mybir.AluOpType.add
COPY = mybir.ActivationFunctionType.Copy

P = 128
PACK = 4
ROWS = 32
SIDE = 4
SETS = 2
W = 128
SPLIT = 80
RUN = 4
TILE_ORDER = (0, 2, 1, 3)


def tile_rows_win_ssd_kernel(tc, kT, qT, dk, t, v, S, dq, out):
    nc = tc.nc
    with ExitStack() as ctx:
        sb = ctx.enter_context(tc.tile_pool(name="sb", bufs=1))
        ps = ctx.enter_context(tc.psum_pool(name="ps", bufs=1))
        ctx.enter_context(tc.manual_schedule())

        def load_packed(src, s, name):
            raw = sb.tile([P, PACK, W], F32, name=name + "_raw%d" % s)
            nc.sync.dma_start(
                out=raw[:],
                in_=src[SIDE * s : SIDE * (s + 1)].rearrange("g (p j) w -> (g p) j w", j=PACK),
            )
            return raw

        def load_decay(s):
            raw = sb.tile([P, SIDE, W], F32, name="dk_raw%d" % s)
            nc.sync.dma_start(out=raw[:], in_=dk[SIDE * s : SIDE * (s + 1)].rearrange("g i q -> i g q"))
            return raw

        def interleave(raw, name, vector_cols):
            grouped = sb.tile([P, W, PACK], BF16, name=name + "_grp", align_bytes=64)
            src = raw[:, :, :].rearrange("p j (c i) -> p c j i", i=RUN)
            dst = grouped[:].rearrange("p (c i) j -> p c j i", i=RUN)
            cut = vector_cols // RUN
            if vector_cols > 0:
                nc.vector.tensor_copy(out=dst[:, 0:cut], in_=src[:, 0:cut])
            if vector_cols < W:
                nc.scalar.copy(out=dst[:, cut:], in_=src[:, cut:])
            return grouped

        def quantize(grouped, name):
            codes = sb.tile([P, W], U32, name=name + "_codes", align_bytes=64)
            scales = sb.tile([P, W], U8, name=name + "_scales", align_bytes=64)
            nc.vector.quantize_mx(
                out=codes[:].bitcast(FP8X4),
                scales=scales[:],
                in_=grouped[:].rearrange("p w j -> p (w j)"),
            )
            return codes, scales

        banks = []
        for s in range(SETS):
            row = []
            for r in range(SIDE):
                bank = ps.tile([P, 4, W], F32, name="bank%d_%d" % (s, r))
                row.append(bank)
            banks.append(row)

        def products(s, slot, stationary, moving, order):
            for r in order:
                rows = slice(ROWS * r, ROWS * (r + 1))
                nc.tensor.matmul_mx(
                    out=banks[s][r][:, slot, :],
                    lhsT=stationary[0][rows, :].bitcast(FP8X4),
                    lhsT_scale=stationary[1][rows, :],
                    rhs=moving[0][rows, :].bitcast(FP8X4),
                    rhs_scale=moving[1][rows, :],
                    start=True,
                    stop=True,
                )

        t_rows = sb.tile([P, G, ROWS], F32, name="t_rows", align_bytes=64)
        t_cols = sb.tile([P, G, ROWS], F32, name="t_cols", align_bytes=64)
        dq_rows = sb.tile([P, G, ROWS], F32, name="dq_rows", align_bytes=64)
        dq_cols = sb.tile([P, G, ROWS], F32, name="dq_cols", align_bytes=64)
        nc.vector.memset(t_rows[:], 0.0)
        nc.vector.memset(dq_rows[:], 0.0)

        def load_rows(rows, src):
            nc.sync.dma_start(out=rows[0:P:ROWS], in_=src.rearrange("g (a b) o -> a g (b o)", b=ROWS))

        def turn(cols, rows):
            nc.vector.transpose(out=cols[:].rearrange("p g b -> p (g b)"), in_=rows[:].rearrange("p g b -> p (g b)"))

        p_rows = sb.tile([P, SIDE, SETS * W], BF16, name="p_rows")
        p_raw = sb.tile([P, PACK, SETS * W], BF16, name="p_raw")
        carried = []
        res = []
        for s in range(SETS):
            c_tile = sb.tile([P, SIDE, W], F32, name="carried%d" % s)
            r_tile = sb.tile([P, SIDE, W], F32, name="res%d" % s)
            carried.append(c_tile)
            res.append(r_tile)

        def weights(s, r):
            nc.vector.scalar_tensor_tensor(
                out=p_rows[:, r, s * W : (s + 1) * W],
                in0=banks[s][r][:, 0, :],
                scalar=t_cols[:, SIDE * s + r, 0:1],
                in1=decay[s][:, r, :],
                op0=MULT,
                op1=MULT,
            )

        def scale_state_term(s):
            for r in range(SIDE):
                nc.scalar.activation(
                    out=carried[s][:, r, :], in_=banks[s][r][:, 1, :], func=COPY, scale=dq_cols[:, SIDE * s + r, 0:1]
                )

        def add(s, r):
            nc.vector.tensor_tensor(out=res[s][:, r, :], in0=banks[s][r][:, 2, :], in1=carried[s][:, r, :], op=ADD)

        def store(s, r0, r1):
            g0 = SIDE * s
            nc.sync.dma_start(out=out[g0 + r0 : g0 + r1].rearrange("g q e -> q g e"), in_=res[s][:, r0:r1, :])

        k_raw0 = load_packed(kT, 0, "k")
        q_raw0 = load_packed(qT, 0, "q")
        load_rows(t_rows, t)
        k_raw1 = load_packed(kT, 1, "k")
        q_raw1 = load_packed(qT, 1, "q")
        decay = [load_decay(0), load_decay(1)]
        s_raw0 = load_packed(S, 0, "s")
        s_raw1 = load_packed(S, 1, "s")
        load_rows(dq_rows, dq)
        v_raw0 = load_packed(v, 0, "v")
        v_raw1 = load_packed(v, 1, "v")

        k_grp0 = interleave(k_raw0, "k0", W)
        q_grp0 = interleave(q_raw0, "q0", 0)
        k_mx0 = quantize(k_grp0, "k0")
        turn(t_cols, t_rows)
        k_grp1 = interleave(k_raw1, "k1", W)
        q_mx0 = quantize(q_grp0, "q0")
        products(0, 0, k_mx0, q_mx0, TILE_ORDER)
        q_grp1 = interleave(q_raw1, "q1", SPLIT)
        k_mx1 = quantize(k_grp1, "k1")
        q_mx1 = quantize(q_grp1, "q1")
        products(1, 0, k_mx1, q_mx1, TILE_ORDER)
        for r in TILE_ORDER:
            weights(0, r)
        for r in TILE_ORDER:
            weights(1, r)
            nc.sync.dma_start(out=p_raw[ROWS * r : ROWS * (r + 1)], in_=p_rows[:, r, :])

        s_grp0 = interleave(s_raw0, "s0", 0)
        s_grp1 = interleave(s_raw1, "s1", W)
        s_mx0 = quantize(s_grp0, "s0")
        products(0, 1, q_mx0, s_mx0, range(SIDE))
        s_mx1 = quantize(s_grp1, "s1")
        products(1, 1, q_mx1, s_mx1, range(SIDE))
        v_grp0 = interleave(v_raw0, "v0", 0)
        turn(dq_cols, dq_rows)
        v_grp1 = interleave(v_raw1, "v1", W)
        v_mx0 = quantize(v_grp0, "v0")
        scale_state_term(0)
        v_mx1 = quantize(v_grp1, "v1")
        p_grp0 = interleave(p_raw[:, :, 0:W], "p0", SPLIT)
        p_grp1 = interleave(p_raw[:, :, W : 2 * W], "p1", 0)
        scale_state_term(1)
        p_mx0 = quantize(p_grp0, "p0")
        products(0, 2, p_mx0, v_mx0, range(SIDE))
        p_mx1 = quantize(p_grp1, "p1")
        products(1, 2, p_mx1, v_mx1, range(SIDE))
        for s in range(SETS):
            for r in range(SIDE):
                add(s, r)
                if r % 2 == 1:
                    store(s, r - 1, r + 1)
